import numpy as np
import ml_dtypes


def mxq(x, axis, fmt="e4m3"):
    dtype, down = {"e4m3": (ml_dtypes.float8_e4m3fn, 7), "e5m2": (ml_dtypes.float8_e5m2, 14)}[fmt]
    v = np.moveaxis(np.asarray(x, np.float32).astype(ml_dtypes.bfloat16).astype(np.float64), axis, -1)
    blocks = v.reshape(v.shape[:-1] + (-1, 32))
    amax = np.abs(blocks).max(-1, keepdims=True)
    byte = np.maximum(np.where(amax > 0, np.frexp(amax)[1] - 1 + 127, 0) - down, 1)
    scale = np.exp2(byte - 127.0)
    codes = (blocks / scale).astype(np.float32).astype(dtype).astype(np.float64)
    return np.moveaxis((codes * scale).reshape(v.shape), -1, axis)


WIDE = False


def mx_kscale(k):
    if not WIDE:
        return np.ones(k)
    levels = np.array([10, -10, 5, -5, 0])
    if k % 512:
        return np.exp2(np.random.permutation(np.resize(levels, k // 32))).repeat(32)
    a = np.empty((k // 512, 16))
    for p in range(k // 512):
        a[p, :8] = np.random.permutation(np.resize(levels, 8))
        for g in range(8):
            far = levels[np.abs(levels - a[p, g]) >= 10]
            a[p, g + 8] = far[np.random.randint(len(far))]
    return np.exp2(a.ravel()).repeat(32)


BF16 = ml_dtypes.bfloat16


def bf(x):
    return np.asarray(x, np.float32).astype(BF16)


def f64(x):
    return np.asarray(x).astype(np.float64)


E2M1 = np.array([0.0, 0.5, 1.0, 1.5, 2.0, 3.0, 4.0, 6.0, -0.0, -0.5, -1.0, -1.5, -2.0, -3.0, -4.0, -6.0])


def pack_weight(w, fmt):
    k, n = w.shape
    w = f64(bf(w)).reshape(k // 32, 32, n)
    amax = np.abs(w).max(1)
    if fmt == "e4m3":
        byte = np.frexp(amax)[1] - 1 + 127 - 7
    else:
        mant, ex = np.frexp(amax / 6.0)
        byte = np.where(mant > 0.5, ex, ex - 1) + 127
    byte = np.clip(np.where(amax > 0, byte, 1), 1, 254)
    scaled = (w * np.exp2(127.0 - byte)[:, None, :]).reshape(k, n).astype(np.float32)
    by_word = np.ascontiguousarray(scaled.reshape(k // 512, 128, 4, n).transpose(0, 1, 3, 2))
    if fmt == "e4m3":
        words = by_word.astype(ml_dtypes.float8_e4m3fn).view(np.uint8)
    else:
        c = by_word.astype(ml_dtypes.float4_e2m1fn).view(np.uint8) & 0xF
        words = c[..., 0::2] | (c[..., 1::2] << 4)
    return np.ascontiguousarray(words), np.ascontiguousarray(byte.astype(np.uint8).reshape(k // 512, 16, n))


def unpack_weight(words, scales, fmt):
    g, p, n, _ = words.shape
    if fmt == "e4m3":
        vals = np.ascontiguousarray(words).view(ml_dtypes.float8_e4m3fn).astype(np.float64)
    else:
        nib = np.empty((g, p, n, 4), np.uint8)
        nib[..., 0::2] = words & 0xF
        nib[..., 1::2] = words >> 4
        vals = E2M1[nib]
    vals = vals * np.repeat(np.exp2(scales.astype(np.float64) - 127.0), 8, axis=1)[..., None]
    return vals.transpose(0, 1, 3, 2).reshape(g * 512, n)
def pack4(w):
    words, scales = pack_weight(w, "e2m1")
    return words.reshape(words.shape[0], 128, -1), scales


def unpack4(words, scales):
    return unpack_weight(words.reshape(words.shape[0], 128, -1, 2), scales, "e2m1")


B, D = 1536, 1024


def setup_inputs():
    s, t = mx_kscale(D), mx_kscale(D)
    st = np.concatenate([s, t])
    z = bf(np.random.standard_normal((2 * D, B)) * st[:, None])
    units = bf((1 + 0.1 * np.random.standard_normal(2 * D)) / st)
    a = np.random.standard_normal((D, D)) / (3 * np.sqrt(D)) / s[:, None] * t
    v = np.random.standard_normal((D, D)) / (3 * np.sqrt(D)) / t[:, None] * s
    a_words, a_scales = pack4(a)
    v_words, v_scales = pack4(v)
    return {"z": z, "units": units,
            "a_words": a_words, "a_scales": a_scales,
            "v_words": v_words, "v_scales": v_scales}


def reference(z, units, a_words, a_scales, v_words, v_scales):
    state, u = f64(z), f64(units)[:, None]
    x, y = state[:D], state[D:]
    a = unpack4(a_words, a_scales)
    v = unpack4(v_words, v_scales)
    y_half = y - (a.T @ mxq(x, 0, "e4m3"))
    x_new = x + (v.T @ mxq(y_half, 0, "e4m3"))
    y_new = y_half - (a.T @ mxq(x_new, 0, "e4m3"))
    return x_new * u[:D], y_new * u[D:]

@@ -1,0 +1,229 @@
+from contextlib import ExitStack
+
+import concourse.mybir as mybir
+
+D, B = 1024, 1536
+FLOPS = 3 * 2 * D * D * B
+
+F32 = mybir.dt.float32
+BF16 = mybir.dt.bfloat16
+I32 = mybir.dt.int32
+U32 = mybir.dt.uint32
+U8 = mybir.dt.uint8
+FP8X4 = mybir.dt.float8_e4m3fn_x4
+FP4X4 = mybir.dt.float4_e2m1fn_x4
+ALU = mybir.AluOpType
+COPY = mybir.ActivationFunctionType.Copy
+
+P = 128
+PACK = 4
+GROUP = P * PACK
+GROUPS = D // GROUP
+N = 512
+TILES = B // N
+STAGES = 3
+SLOTS = STAGES * TILES
+BANKS = GROUPS * PACK
+RUN = 4
+QUANT_AFTER = 4
+
+
+def tile_leapfrog_kick_drift_kick_t2_kernel(tc, z, units, a_words, a_scales, v_words, v_scales, out_0, out_1):
+    nc = tc.nc
+
+    def rows_of(dram, base, g, j):
+        return dram[base + g * GROUP : base + (g + 1) * GROUP, j * N : (j + 1) * N].rearrange("(p t) n -> p t n", t=PACK)
+
+    with ExitStack() as ctx:
+        keep = ctx.enter_context(tc.tile_pool(name="keep", bufs=1))
+        ring = ctx.enter_context(tc.tile_pool(name="ring", bufs=2))
+        psum = ctx.enter_context(tc.psum_pool(name="psum", bufs=BANKS))
+        ctx.enter_context(tc.manual_schedule())
+
+        x = [[keep.tile([P, PACK, N], BF16, name="x%d%d" % (j, g)) for g in range(GROUPS)] for j in range(TILES)]
+        y = [[keep.tile([P, PACK, N], BF16, name="y%d%d" % (j, g)) for g in range(GROUPS)] for j in range(TILES)]
+        y_scaled = [[keep.tile([P, PACK, N], F32, name="ys%d%d" % (j, g)) for g in range(GROUPS)] for j in range(TILES)]
+        raw_words = [[keep.tile([P, GROUPS, 2 * GROUP], U8, name="rw%d%d" % (w, h)) for h in range(GROUPS)] for w in range(2)]
+        words = [[keep.tile([P, GROUPS, 2 * GROUP], U8, name="w%d%d" % (w, h), align_bytes=256) for h in range(GROUPS)] for w in range(2)]
+        raw_scales = [keep.tile([P, GROUPS * D], U8, name="rs%d" % w) for w in range(2)]
+        scales = [keep.tile([P, GROUPS * D], U8, name="s%d" % w, align_bytes=256) for w in range(2)]
+        unit_bf = keep.tile([P, 2 * GROUPS, PACK], BF16)
+        unit = keep.tile([P, 2 * BANKS], F32)
+        minus_unit_y = keep.tile([P, BANKS], F32)
+
+        def load_words(w, h):
+            src = (a_words, v_words)[w][:, :, h * 2 * GROUP : (h + 1) * 2 * GROUP].rearrange("g p n -> p g n")
+            nc.sync.dma_start(out=raw_words[w][h][:].bitcast(I32), in_=src.bitcast(I32))
+
+        def load_scales(w, queue):
+            for q in range(4):
+                src = (a_scales, v_scales)[w][:, 4 * q : 4 * q + 4, :].rearrange("g r n -> r g n")
+                dst = raw_scales[w][32 * q : 32 * q + 4, :].rearrange("r (g n) -> r g n", g=GROUPS)
+                queue.dma_start(out=dst.bitcast(I32), in_=src.bitcast(I32))
+
+        def load_x(j, g):
+            nc.sync.dma_start(out=x[j][g][:], in_=rows_of(z, 0, g, j))
+
+        def load_y(j, g):
+            nc.sync.dma_start(out=y[j][g][:], in_=rows_of(z, D, g, j))
+
+        def sort_words(w, h):
+            nc.vector.tensor_copy(
+                out=words[w][h][:].rearrange("p g (t m b) -> p g t m b", t=PACK, b=2),
+                in_=raw_words[w][h][:].rearrange("p g (m t b) -> p g t m b", t=PACK, b=2),
+            )
+
+        def sort_scales(w):
+            nc.vector.tensor_copy(
+                out=scales[w][:].rearrange("p (c t m) -> p c t m", t=PACK, m=P),
+                in_=raw_scales[w][:].rearrange("p (c m t) -> p c t m", t=PACK, m=P),
+            )
+
+        nc.vector.memset(raw_scales[0][:].bitcast(I32), 0)
+        nc.gpsimd.memset(raw_scales[1][:].bitcast(I32), 0)
+        nc.scalar.dma_start(out=unit_bf[:], in_=units.rearrange("(c p t) -> p c t", p=P, t=PACK))
+        load_scales(0, nc.scalar)
+        load_x(0, 0)
+        load_words(0, 0)
+        load_words(0, 1)
+        load_x(0, 1)
+        load_words(1, 0)
+        load_words(1, 1)
+        load_scales(1, nc.sync)
+        for j in range(TILES):
+            for g in range(GROUPS):
+                if j + 1 < TILES:
+                    load_x(j + 1, g)
+                load_y(j, g)
+
+        nc.scalar.activation(out=unit[:], in_=unit_bf[:].rearrange("p c t -> p (c t)"), func=COPY)
+        nc.scalar.activation(out=minus_unit_y[:], in_=unit[:, BANKS:], func=COPY, scale=-1.0)
+
+        results = {}
+        packed = {}
+        codes = {}
+        code_scales = {}
+        staged = {}
+
+        def interleave(k):
+            tile = ring.tile([P, GROUPS, N, PACK], BF16, name="packed", bufs=2, align_bytes=256)
+            packed[k] = tile
+            for g in range(GROUPS):
+                src = x[k][g] if k < TILES else results[k - TILES, g]
+                nc.scalar.copy(
+                    out=tile[:, g].rearrange("p (c i) t -> p c t i", i=RUN),
+                    in_=src[:].rearrange("p t (c i) -> p c t i", i=RUN),
+                )
+
+        def new_codes(k):
+            code_tile = ring.tile([P, GROUPS * N], U32, name="codes", bufs=3, align_bytes=256)
+            scale_tile = ring.tile([P, GROUPS * N], U8, name="code_scales", bufs=3, align_bytes=256)
+            codes[k] = code_tile
+            code_scales[k] = scale_tile
+
+        def quantize(k, g0, g1):
+            nc.vector.quantize_mx(
+                out=codes[k][:, g0 * N : g1 * N].bitcast(FP8X4),
+                scales=code_scales[k][:, g0 * N : g1 * N],
+                in_=packed[k][:, g0:g1].rearrange("p g n t -> p (g n t)"),
+            )
+
+        def matmul_pass(k, acc, h, t, g):
+            w = (k // TILES) % 2
+            first = (g * BANKS + h * PACK + t) * P
+            nc.tensor.matmul_mx(
+                out=acc[:],
+                lhsT=words[w][h][:, g, t * 2 * P : (t + 1) * 2 * P].bitcast(FP4X4),
+                lhsT_scale=scales[w][:, first : first + P],
+                rhs=codes[k][:, g * N : (g + 1) * N].bitcast(FP8X4),
+                rhs_scale=code_scales[k][:, g * N : (g + 1) * N],
+                start=(g == 0),
+                stop=(g == GROUPS - 1),
+            )
+
+        def store(dram, tile, h, j, t0, t1):
+            nc.sync.dma_start(out=rows_of(dram, 0, h, j)[:, t0:t1, :], in_=tile[:, t0:t1, :])
+
+        def apply_units(k, h, t):
+            stage, j = divmod(k, TILES)
+            if stage == 0:
+                dst = y_scaled[j][h]
+                col = BANKS + h * PACK + t
+            else:
+                if t == 0:
+                    out_tile = ring.tile([P, PACK, N], F32, name="staged", bufs=4)
+                    staged[k, h] = out_tile
+                dst = staged[k, h]
+                col = h * PACK + t
+            nc.gpsimd.tensor_scalar(
+                out=dst[:, t, :], in0=results[k, h][:, t, :], scalar1=unit[:, col : col + 1], scalar2=0.0, op0=ALU.mult, op1=ALU.add
+            )
+            if stage == 1 and t % 2 == 1:
+                store(out_0, dst, h, j, t - 1, t + 1)
+
+        interleave(0)
+        interleave(1)
+        new_codes(0)
+        sort_words(0, 0)
+        sort_words(0, 1)
+        sort_scales(0)
+        quantize(0, 0, 1)
+        sort_words(1, 0)
+        quantize(0, 1, 2)
+        sort_words(1, 1)
+        sort_scales(1)
+
+        pending = []
+        for k in range(SLOTS):
+            stage, j = divmod(k, TILES)
+            if k + 2 < SLOTS:
+                interleave(k + 2)
+            if k == SLOTS - 2:
+                for h in range(GROUPS):
+                    for t in range(PACK):
+                        col = BANKS + h * PACK + t
+                        row = y_scaled[TILES - 1][h][:, t, :]
+                        nc.scalar.activation(out=row, in_=row, func=COPY, scale=unit[:, col : col + 1])
+            for h in range(GROUPS):
+                if k == TILES - 1:
+                    results[k, h] = y_scaled[j][h]
+                elif stage < 2:
+                    result_tile = ring.tile([P, PACK, N], F32, name="result", bufs=5)
+                    results[k, h] = result_tile
+                accs = []
+                if k == 0:
+                    for t in range(PACK):
+                        acc = psum.tile([P, N], F32, name="acc")
+                        accs.append(acc)
+                        matmul_pass(k, acc, h, t, 0)
+                for t in range(PACK):
+                    b = h * PACK + t
+                    if k == 0:
+                        acc = accs[t]
+                        matmul_pass(k, acc, h, t, 1)
+                    else:
+                        acc = psum.tile([P, N], F32, name="acc")
+                        for g in range(GROUPS):
+                            matmul_pass(k, acc, h, t, g)
+                    if stage == 0:
+                        nc.vector.tensor_tensor(out=results[k, h][:, t, :], in0=y[j][h][:, t, :], in1=acc[:], op=ALU.subtract)
+                    elif stage == 1:
+                        nc.vector.tensor_tensor(out=results[k, h][:, t, :], in0=x[j][h][:, t, :], in1=acc[:], op=ALU.add)
+                    else:
+                        row = y_scaled[j][h][:, t, :]
+                        nc.vector.scalar_tensor_tensor(
+                            out=row, in0=acc[:], scalar=minus_unit_y[:, b : b + 1], in1=row, op0=ALU.mult, op1=ALU.add
+                        )
+                        if k == SLOTS - 1 and h == GROUPS - 1 and t >= 2:
+                            store(out_1, y_scaled[j][h], h, j, t, t + 1)
+                        elif t % 2 == 1:
+                            store(out_1, y_scaled[j][h], h, j, t - 1, t + 1)
+                    if stage < 2 and k != TILES - 1:
+                        pending.append((k, h, t))
+                    if pending and t != PACK - 1:
+                        apply_units(*pending[0])
+                        pending.remove(pending[0])
+                    if b == QUANT_AFTER and k + 1 < SLOTS:
+                        new_codes(k + 1)
+                        quantize(k + 1, 0, GROUPS)
+        assert not pending

@@ -25,7 +25,18 @@ STAGES = 3
 SLOTS = STAGES * TILES
 BANKS = GROUPS * PACK
 RUN = 4
-QUANT_AFTER = 4
+SCALE_ROWS = 4
+ORDER = sorted(((s, j) for s in range(STAGES) for j in range(TILES)), key=lambda sj: 3 * sj[0] + 2 * sj[1])
+SLOT_OF = {sj: k for k, sj in enumerate(ORDER)}
+
+
+def source_slot(k):
+    stage, j = ORDER[k]
+    return SLOT_OF[stage - 1, j] if stage > 0 else None
+
+
+def quantize_after(k):
+    return 5 if k == 0 or source_slot(k + 1) == k - 1 else 4
 
 
 def tile_leapfrog_kick_drift_kick_t2_kernel(tc, z, units, a_words, a_scales, v_words, v_scales, out_0, out_1):
@@ -42,10 +53,11 @@ def tile_leapfrog_kick_drift_kick_t2_kernel(tc, z, units, a_words, a_scales, v_w
 
         x = [[keep.tile([P, PACK, N], BF16, name="x%d%d" % (j, g)) for g in range(GROUPS)] for j in range(TILES)]
         y = [[keep.tile([P, PACK, N], BF16, name="y%d%d" % (j, g)) for g in range(GROUPS)] for j in range(TILES)]
-        y_scaled = [[keep.tile([P, PACK, N], F32, name="ys%d%d" % (j, g)) for g in range(GROUPS)] for j in range(TILES)]
+        momenta = [[keep.tile([P, PACK, N], F32, name="m%d%d" % (j, g)) for g in range(GROUPS)] for j in range(TILES)]
+        early = [keep.tile([P, N], F32, name="early%d" % j) for j in range(TILES)]
         raw_words = [[keep.tile([P, GROUPS, 2 * GROUP], U8, name="rw%d%d" % (w, h)) for h in range(GROUPS)] for w in range(2)]
         words = [[keep.tile([P, GROUPS, 2 * GROUP], U8, name="w%d%d" % (w, h), align_bytes=256) for h in range(GROUPS)] for w in range(2)]
-        raw_scales = [keep.tile([P, GROUPS * D], U8, name="rs%d" % w) for w in range(2)]
+        raw_scales = keep.tile([P, GROUPS * D], U8, name="rs")
         scales = [keep.tile([P, GROUPS * D], U8, name="s%d" % w, align_bytes=256) for w in range(2)]
         unit_bf = keep.tile([P, 2 * GROUPS, PACK], BF16)
         unit = keep.tile([P, 2 * BANKS], F32)
@@ -57,8 +69,9 @@ def tile_leapfrog_kick_drift_kick_t2_kernel(tc, z, units, a_words, a_scales, v_w
 
         def load_scales(w, queue):
             for q in range(4):
+                first = 32 * q + SCALE_ROWS * w
                 src = (a_scales, v_scales)[w][:, 4 * q : 4 * q + 4, :].rearrange("g r n -> r g n")
-                dst = raw_scales[w][32 * q : 32 * q + 4, :].rearrange("r (g n) -> r g n", g=GROUPS)
+                dst = raw_scales[first : first + SCALE_ROWS, :].rearrange("r (g n) -> r g n", g=GROUPS)
                 queue.dma_start(out=dst.bitcast(I32), in_=src.bitcast(I32))
 
         def load_x(j, g):
@@ -73,55 +86,43 @@ def tile_leapfrog_kick_drift_kick_t2_kernel(tc, z, units, a_words, a_scales, v_w
                 in_=raw_words[w][h][:].rearrange("p g (m t b) -> p g t m b", t=PACK, b=2),
             )
 
-        def sort_scales(w):
+        def sort_scales():
             nc.vector.tensor_copy(
-                out=scales[w][:].rearrange("p (c t m) -> p c t m", t=PACK, m=P),
-                in_=raw_scales[w][:].rearrange("p (c m t) -> p c t m", t=PACK, m=P),
+                out=scales[0][:].rearrange("p (c t m) -> p c t m", t=PACK, m=P),
+                in_=raw_scales[:].rearrange("p (c m t) -> p c t m", t=PACK, m=P),
             )
 
-        nc.vector.memset(raw_scales[0][:].bitcast(I32), 0)
-        nc.gpsimd.memset(raw_scales[1][:].bitcast(I32), 0)
-        nc.scalar.dma_start(out=unit_bf[:], in_=units.rearrange("(c p t) -> p c t", p=P, t=PACK))
-        load_scales(0, nc.scalar)
-        load_x(0, 0)
-        load_words(0, 0)
-        load_words(0, 1)
-        load_x(0, 1)
-        load_words(1, 0)
-        load_words(1, 1)
-        load_scales(1, nc.sync)
-        for j in range(TILES):
-            for g in range(GROUPS):
-                if j + 1 < TILES:
-                    load_x(j + 1, g)
-                load_y(j, g)
-
-        nc.scalar.activation(out=unit[:], in_=unit_bf[:].rearrange("p c t -> p (c t)"), func=COPY)
-        nc.scalar.activation(out=minus_unit_y[:], in_=unit[:, BANKS:], func=COPY, scale=-1.0)
+        def move_v_scales():
+            for q in range(4):
+                nc.sync.dma_start(
+                    out=scales[1][32 * q : 32 * q + SCALE_ROWS, :].bitcast(I32),
+                    in_=scales[0][32 * q + SCALE_ROWS : 32 * q + 2 * SCALE_ROWS, :].bitcast(I32),
+                )
 
         results = {}
         packed = {}
         codes = {}
         code_scales = {}
         staged = {}
+        interleaved = set()
 
-        def interleave(k):
-            tile = ring.tile([P, GROUPS, N, PACK], BF16, name="packed", bufs=2, align_bytes=256)
-            packed[k] = tile
-            for g in range(GROUPS):
-                src = x[k][g] if k < TILES else results[k - TILES, g]
-                nc.scalar.copy(
-                    out=tile[:, g].rearrange("p (c i) t -> p c t i", i=RUN),
-                    in_=src[:].rearrange("p t (c i) -> p c t i", i=RUN),
-                )
-
-        def new_codes(k):
-            code_tile = ring.tile([P, GROUPS * N], U32, name="codes", bufs=3, align_bytes=256)
-            scale_tile = ring.tile([P, GROUPS * N], U8, name="code_scales", bufs=3, align_bytes=256)
-            codes[k] = code_tile
-            code_scales[k] = scale_tile
+        def interleave(k, g):
+            if g == 0:
+                tile = ring.tile([P, GROUPS, N, PACK], BF16, name="packed", bufs=3, align_bytes=256)
+                packed[k] = tile
+            src = x[ORDER[k][1]][g] if source_slot(k) is None else results[source_slot(k), g]
+            nc.scalar.copy(
+                out=packed[k][:, g].rearrange("p (c i) t -> p c t i", i=RUN),
+                in_=src[:].rearrange("p t (c i) -> p c t i", i=RUN),
+            )
+            interleaved.add((source_slot(k), g))
 
         def quantize(k, g0, g1):
+            if g0 == 0:
+                code_tile = ring.tile([P, GROUPS * N], U32, name="codes", bufs=3, align_bytes=256)
+                scale_tile = ring.tile([P, GROUPS * N], U8, name="code_scales", bufs=3, align_bytes=256)
+                codes[k] = code_tile
+                code_scales[k] = scale_tile
             nc.vector.quantize_mx(
                 out=codes[k][:, g0 * N : g1 * N].bitcast(FP8X4),
                 scales=code_scales[k][:, g0 * N : g1 * N],
@@ -129,7 +130,7 @@ def tile_leapfrog_kick_drift_kick_t2_kernel(tc, z, units, a_words, a_scales, v_w
             )
 
         def matmul_pass(k, acc, h, t, g):
-            w = (k // TILES) % 2
+            w = ORDER[k][0] % 2
             first = (g * BANKS + h * PACK + t) * P
             nc.tensor.matmul_mx(
                 out=acc[:],
@@ -141,54 +142,111 @@ def tile_leapfrog_kick_drift_kick_t2_kernel(tc, z, units, a_words, a_scales, v_w
                 stop=(g == GROUPS - 1),
             )
 
-        def store(dram, tile, h, j, t0, t1):
-            nc.sync.dma_start(out=rows_of(dram, 0, h, j)[:, t0:t1, :], in_=tile[:, t0:t1, :])
+        finished = set()
 
-        def apply_units(k, h, t):
-            stage, j = divmod(k, TILES)
-            if stage == 0:
-                dst = y_scaled[j][h]
-                col = BANKS + h * PACK + t
-            else:
-                if t == 0:
+        def finish(stage, j, b):
+            h, t = divmod(b, PACK)
+            dram, tile = (out_0, staged[j, h]) if stage == 1 else (out_1, momenta[j][h])
+            finished.add((stage, j, b))
+            if SLOT_OF[stage, j] == SLOTS - 1 and b >= BANKS - 2:
+                nc.sync.dma_start(out=rows_of(dram, 0, h, j)[:, t : t + 1, :], in_=tile[:, t : t + 1, :])
+            elif (stage, j, b ^ 1) in finished:
+                t0 = t - t % 2
+                nc.sync.dma_start(out=rows_of(dram, 0, h, j)[:, t0 : t0 + 2, :], in_=tile[:, t0 : t0 + 2, :])
+
+        prescaled = {}
+
+        def scale_rows(on_scalar, stage, j, b, aside=False):
+            h, t = divmod(b, PACK)
+            if stage == 1:
+                if (j, h) not in staged:
                     out_tile = ring.tile([P, PACK, N], F32, name="staged", bufs=4)
-                    staged[k, h] = out_tile
-                dst = staged[k, h]
-                col = h * PACK + t
-            nc.gpsimd.tensor_scalar(
-                out=dst[:, t, :], in0=results[k, h][:, t, :], scalar1=unit[:, col : col + 1], scalar2=0.0, op0=ALU.mult, op1=ALU.add
-            )
-            if stage == 1 and t % 2 == 1:
-                store(out_0, dst, h, j, t - 1, t + 1)
+                    staged[j, h] = out_tile
+                src, dst, col = results[SLOT_OF[1, j], h][:, t, :], staged[j, h][:, t, :], b
+            else:
+                src = momenta[j][h][:, t, :]
+                dst, col = (early[j][:] if aside else src), BANKS + b
+            if on_scalar:
+                nc.scalar.activation(out=dst, in_=src, func=COPY, scale=unit[:, col : col + 1])
+            else:
+                nc.gpsimd.tensor_scalar(out=dst, in0=src, scalar1=unit[:, col : col + 1], scalar2=0.0, op0=ALU.mult, op1=ALU.add)
+            if stage == 0:
+                prescaled[j, b] = dst
+            else:
+                finish(stage, j, b)
 
-        interleave(0)
-        interleave(1)
-        new_codes(0)
+        nc.vector.memset(raw_scales[:].bitcast(I32), 0)
+        nc.vector.memset(scales[1][:].bitcast(I32), 0)
+        load_words(0, 0)
+        load_x(0, 0)
+        load_scales(0, nc.scalar)
+        load_words(0, 1)
+        load_scales(1, nc.sync)
+        load_x(0, 1)
+        load_words(1, 0)
+        load_words(1, 1)
+        load_x(1, 0)
+        load_y(0, 0)
+        load_x(1, 1)
+        nc.sync.dma_start(out=unit_bf[:], in_=units.rearrange("(c p t) -> p c t", p=P, t=PACK))
+        load_y(0, 1)
+
+        for k in range(2):
+            for g in range(GROUPS):
+                interleave(k, g)
+        nc.scalar.activation(out=unit[:], in_=unit_bf[:].rearrange("p c t -> p (c t)"), func=COPY)
+        nc.scalar.activation(out=minus_unit_y[:], in_=unit_bf[:, GROUPS:].rearrange("p c t -> p (c t)"), func=COPY, scale=-1.0)
         sort_words(0, 0)
         sort_words(0, 1)
-        sort_scales(0)
+        sort_scales()
         quantize(0, 0, 1)
         sort_words(1, 0)
         quantize(0, 1, 2)
         sort_words(1, 1)
-        sort_scales(1)
 
-        pending = []
-        for k in range(SLOTS):
-            stage, j = divmod(k, TILES)
-            if k + 2 < SLOTS:
-                interleave(k + 2)
-            if k == SLOTS - 2:
-                for h in range(GROUPS):
-                    for t in range(PACK):
-                        col = BANKS + h * PACK + t
-                        row = y_scaled[TILES - 1][h][:, t, :]
-                        nc.scalar.activation(out=row, in_=row, func=COPY, scale=unit[:, col : col + 1])
+        move_v_scales()
+        load_y(1, 0)
+        load_x(2, 0)
+        load_y(1, 1)
+        load_x(2, 1)
+        load_y(2, 0)
+        load_y(2, 1)
+
+        outputs_due = []
+        window = {"step": 0, "steps": 0, "left": 0, "open": False}
+
+        def next_prescale(k):
+            for j in range(TILES - 1):
+                if SLOT_OF[2, j] > k:
+                    for b in range(BANKS):
+                        kept = b == quantize_after(SLOT_OF[2, j])
+                        if (j, b) not in prescaled and not kept and (SLOT_OF[0, j], b // PACK) in interleaved:
+                            return (0, j, b)
+            return None
+
+        def gpsimd_turn(k, newest):
+            job = None
+            if not window["open"]:
+                job = newest
+            elif window["step"] % 3 != 0 and window["step"] <= window["steps"] - 2:
+                job = outputs_due[0] if outputs_due else next_prescale(k)
+            if job is not None and window["left"] > 0:
+                if job in outputs_due:
+                    outputs_due.remove(job)
+                scale_rows(False, *job, aside=(job[0] == 0 and not window["open"]))
+                window["open"] = True
+                window["left"] = window["left"] - 1
+
+        for k, (stage, j) in enumerate(ORDER):
+            ahead = k + 2
+            if ahead < SLOTS and source_slot(ahead) != k:
+                for g in range(GROUPS):
+                    interleave(ahead, g)
             for h in range(GROUPS):
-                if k == TILES - 1:
-                    results[k, h] = y_scaled[j][h]
-                elif stage < 2:
-                    result_tile = ring.tile([P, PACK, N], F32, name="result", bufs=5)
+                if stage == 0:
+                    results[k, h] = momenta[j][h]
+                elif stage == 1:
+                    result_tile = ring.tile([P, PACK, N], F32, name="result", bufs=4)
                     results[k, h] = result_tile
                 accs = []
                 if k == 0:
@@ -205,25 +263,50 @@ def tile_leapfrog_kick_drift_kick_t2_kernel(tc, z, units, a_words, a_scales, v_w
                         acc = psum.tile([P, N], F32, name="acc")
                         for g in range(GROUPS):
                             matmul_pass(k, acc, h, t, g)
+                    newest = (stage, j, b)
                     if stage == 0:
                         nc.vector.tensor_tensor(out=results[k, h][:, t, :], in0=y[j][h][:, t, :], in1=acc[:], op=ALU.subtract)
                     elif stage == 1:
                         nc.vector.tensor_tensor(out=results[k, h][:, t, :], in0=x[j][h][:, t, :], in1=acc[:], op=ALU.add)
-                    else:
-                        row = y_scaled[j][h][:, t, :]
+                        if j == TILES - 1 and h == 0:
+                            scale_rows(True, stage, j, b)
+                            newest = None
+                        else:
+                            outputs_due.append(newest)
+                    elif (j, b) in prescaled:
                         nc.vector.scalar_tensor_tensor(
-                            out=row, in0=acc[:], scalar=minus_unit_y[:, b : b + 1], in1=row, op0=ALU.mult, op1=ALU.add
+                            out=momenta[j][h][:, t, :],
+                            in0=acc[:],
+                            scalar=minus_unit_y[:, b : b + 1],
+                            in1=prescaled[j, b],
+                            op0=ALU.mult,
+                            op1=ALU.add,
                         )
-                        if k == SLOTS - 1 and h == GROUPS - 1 and t >= 2:
-                            store(out_1, y_scaled[j][h], h, j, t, t + 1)
-                        elif t % 2 == 1:
-                            store(out_1, y_scaled[j][h], h, j, t - 1, t + 1)
-                    if stage < 2 and k != TILES - 1:
-                        pending.append((k, h, t))
-                    if pending and t != PACK - 1:
-                        apply_units(*pending[0])
-                        pending.remove(pending[0])
-                    if b == QUANT_AFTER and k + 1 < SLOTS:
-                        new_codes(k + 1)
+                        finish(stage, j, b)
+                        newest = None
+                    else:
+                        row = momenta[j][h][:, t, :]
+                        nc.vector.tensor_tensor(out=row, in0=row, in1=acc[:], op=ALU.subtract)
+                        outputs_due.append(newest)
+                    if t == PACK - 1 and ahead < SLOTS and source_slot(ahead) == k:
+                        interleave(ahead, h)
+                    window["step"] = window["step"] + 1
+                    if k + 1 < SLOTS and b == quantize_after(k):
                         quantize(k + 1, 0, GROUPS)
-        assert not pending
+                        if k + 2 < SLOTS:
+                            steps = BANKS - b + quantize_after(k + 1)
+                        else:
+                            steps = 2 * BANKS
+                            for job in [due for due in outputs_due if due != newest]:
+                                outputs_due.remove(job)
+                                scale_rows(True, *job)
+                            for rest in range(BANKS):
+                                if (TILES - 1, rest) not in prescaled:
+                                    scale_rows(True, 0, TILES - 1, rest)
+                        window["step"] = 0
+                        window["steps"] = steps
+                        window["left"] = 2 * steps // 3
+                        window["open"] = False
+                    gpsimd_turn(k, newest)
+        assert not outputs_due
+        assert len(finished) == 2 * TILES * BANKS

@@ -26,7 +26,8 @@ SLOTS = STAGES * TILES
 BANKS = GROUPS * PACK
 RUN = 4
 SCALE_ROWS = 4
-ORDER = sorted(((s, j) for s in range(STAGES) for j in range(TILES)), key=lambda sj: 3 * sj[0] + 2 * sj[1])
+ORDER = [(0, 0), (0, 1), (1, 0), (0, 2), (1, 1), (1, 2), (2, 0), (2, 1), (2, 2)]
+PIECE = N // 2
 SLOT_OF = {sj: k for k, sj in enumerate(ORDER)}
 
 
@@ -54,8 +55,11 @@ def tile_leapfrog_kick_drift_kick_t2_kernel(tc, z, units, a_words, a_scales, v_w
         x = [[keep.tile([P, PACK, N], BF16, name="x%d%d" % (j, g)) for g in range(GROUPS)] for j in range(TILES)]
         y = [[keep.tile([P, PACK, N], BF16, name="y%d%d" % (j, g)) for g in range(GROUPS)] for j in range(TILES)]
         momenta = [[keep.tile([P, PACK, N], F32, name="m%d%d" % (j, g)) for g in range(GROUPS)] for j in range(TILES)]
-        early = [keep.tile([P, N], F32, name="early%d" % j) for j in range(TILES)]
-        raw_words = [[keep.tile([P, GROUPS, 2 * GROUP], U8, name="rw%d%d" % (w, h)) for h in range(GROUPS)] for w in range(2)]
+        raw_v = ring.tile([P, GROUPS, GROUPS, 2 * GROUP], U8, name="packed_late", bufs=1, align_bytes=256)
+        raw_words = [
+            [keep.tile([P, GROUPS, 2 * GROUP], U8, name="rw%d" % h)[:] for h in range(GROUPS)],
+            [raw_v[:, h] for h in range(GROUPS)],
+        ]
         words = [[keep.tile([P, GROUPS, 2 * GROUP], U8, name="w%d%d" % (w, h), align_bytes=256) for h in range(GROUPS)] for w in range(2)]
         raw_scales = keep.tile([P, GROUPS * D], U8, name="rs")
         scales = [keep.tile([P, GROUPS * D], U8, name="s%d" % w, align_bytes=256) for w in range(2)]
@@ -65,7 +69,7 @@ def tile_leapfrog_kick_drift_kick_t2_kernel(tc, z, units, a_words, a_scales, v_w
 
         def load_words(w, h):
             src = (a_words, v_words)[w][:, :, h * 2 * GROUP : (h + 1) * 2 * GROUP].rearrange("g p n -> p g n")
-            nc.sync.dma_start(out=raw_words[w][h][:].bitcast(I32), in_=src.bitcast(I32))
+            nc.sync.dma_start(out=raw_words[w][h].bitcast(I32), in_=src.bitcast(I32))
 
         def load_scales(w, queue):
             for q in range(4):
@@ -77,13 +81,13 @@ def tile_leapfrog_kick_drift_kick_t2_kernel(tc, z, units, a_words, a_scales, v_w
         def load_x(j, g):
             nc.sync.dma_start(out=x[j][g][:], in_=rows_of(z, 0, g, j))
 
-        def load_y(j, g):
-            nc.sync.dma_start(out=y[j][g][:], in_=rows_of(z, D, g, j))
+        def load_y(j, g, t0=0, t1=PACK):
+            nc.sync.dma_start(out=y[j][g][:, t0:t1, :], in_=rows_of(z, D, g, j)[:, t0:t1, :])
 
         def sort_words(w, h):
             nc.vector.tensor_copy(
                 out=words[w][h][:].rearrange("p g (t m b) -> p g t m b", t=PACK, b=2),
-                in_=raw_words[w][h][:].rearrange("p g (m t b) -> p g t m b", t=PACK, b=2),
+                in_=raw_words[w][h].rearrange("p g (m t b) -> p g t m b", t=PACK, b=2),
             )
 
         def sort_scales():
@@ -104,29 +108,36 @@ def tile_leapfrog_kick_drift_kick_t2_kernel(tc, z, units, a_words, a_scales, v_w
         codes = {}
         code_scales = {}
         staged = {}
-        interleaved = set()
 
-        def interleave(k, g):
-            if g == 0:
-                tile = ring.tile([P, GROUPS, N, PACK], BF16, name="packed", bufs=3, align_bytes=256)
-                packed[k] = tile
-            src = x[ORDER[k][1]][g] if source_slot(k) is None else results[source_slot(k), g]
+        def operand_rows(k, g):
+            return x[ORDER[k][1]][g] if source_slot(k) is None else results[source_slot(k), g]
+
+        def interleave_on_scalar(k, g, n0, n1):
+            if n0 == 0:
+                tile = ring.tile([P, N, PACK], BF16, name="packed_early", bufs=4, align_bytes=256)
+                packed[k, g] = tile
             nc.scalar.copy(
-                out=packed[k][:, g].rearrange("p (c i) t -> p c t i", i=RUN),
-                in_=src[:].rearrange("p t (c i) -> p c t i", i=RUN),
+                out=packed[k, g][:, n0:n1, :].rearrange("p (c i) t -> p c t i", i=RUN),
+                in_=operand_rows(k, g)[:, :, n0:n1].rearrange("p t (c i) -> p c t i", i=RUN),
             )
-            interleaved.add((source_slot(k), g))
 
-        def quantize(k, g0, g1):
-            if g0 == 0:
+        def interleave_on_gpsimd(k):
+            tile = ring.tile([P, N, PACK], BF16, name="packed_late", bufs=1, align_bytes=256)
+            packed[k, 1] = tile
+            nc.gpsimd.tensor_scalar(
+                out=tile[:], in0=operand_rows(k, 1)[:].rearrange("p t n -> p n t"), scalar1=1.0, scalar2=0.0, op0=ALU.mult, op1=ALU.add
+            )
+
+        def quantize(k, g):
+            if g == 0:
                 code_tile = ring.tile([P, GROUPS * N], U32, name="codes", bufs=3, align_bytes=256)
                 scale_tile = ring.tile([P, GROUPS * N], U8, name="code_scales", bufs=3, align_bytes=256)
                 codes[k] = code_tile
                 code_scales[k] = scale_tile
             nc.vector.quantize_mx(
-                out=codes[k][:, g0 * N : g1 * N].bitcast(FP8X4),
-                scales=code_scales[k][:, g0 * N : g1 * N],
-                in_=packed[k][:, g0:g1].rearrange("p g n t -> p (g n t)"),
+                out=codes[k][:, g * N : (g + 1) * N].bitcast(FP8X4),
+                scales=code_scales[k][:, g * N : (g + 1) * N],
+                in_=packed[k, g][:].rearrange("p n t -> p (n t)"),
             )
 
         def matmul_pass(k, acc, h, t, g):
@@ -154,24 +165,23 @@ def tile_leapfrog_kick_drift_kick_t2_kernel(tc, z, units, a_words, a_scales, v_w
                 t0 = t - t % 2
                 nc.sync.dma_start(out=rows_of(dram, 0, h, j)[:, t0 : t0 + 2, :], in_=tile[:, t0 : t0 + 2, :])
 
-        prescaled = {}
+        prescaled = set()
 
-        def scale_rows(on_scalar, stage, j, b, aside=False):
+        def scale_rows(on_scalar, stage, j, b):
             h, t = divmod(b, PACK)
             if stage == 1:
-                if (j, h) not in staged:
+                if t == 0:
                     out_tile = ring.tile([P, PACK, N], F32, name="staged", bufs=4)
                     staged[j, h] = out_tile
                 src, dst, col = results[SLOT_OF[1, j], h][:, t, :], staged[j, h][:, t, :], b
             else:
-                src = momenta[j][h][:, t, :]
-                dst, col = (early[j][:] if aside else src), BANKS + b
+                src, dst, col = momenta[j][h][:, t, :], momenta[j][h][:, t, :], BANKS + b
             if on_scalar:
                 nc.scalar.activation(out=dst, in_=src, func=COPY, scale=unit[:, col : col + 1])
             else:
                 nc.gpsimd.tensor_scalar(out=dst, in0=src, scalar1=unit[:, col : col + 1], scalar2=0.0, op0=ALU.mult, op1=ALU.add)
             if stage == 0:
-                prescaled[j, b] = dst
+                prescaled.add((j, b))
             else:
                 finish(stage, j, b)
 
@@ -186,23 +196,23 @@ def tile_leapfrog_kick_drift_kick_t2_kernel(tc, z, units, a_words, a_scales, v_w
         load_words(1, 0)
         load_words(1, 1)
         load_x(1, 0)
-        load_y(0, 0)
+        load_y(0, 0, 0, PACK // 2)
         load_x(1, 1)
-        nc.sync.dma_start(out=unit_bf[:], in_=units.rearrange("(c p t) -> p c t", p=P, t=PACK))
+        load_y(0, 0, PACK // 2, PACK)
         load_y(0, 1)
+        nc.sync.dma_start(out=unit_bf[:], in_=units.rearrange("(c p t) -> p c t", p=P, t=PACK))
 
-        for k in range(2):
-            for g in range(GROUPS):
-                interleave(k, g)
-        nc.scalar.activation(out=unit[:], in_=unit_bf[:].rearrange("p c t -> p (c t)"), func=COPY)
-        nc.scalar.activation(out=minus_unit_y[:], in_=unit_bf[:, GROUPS:].rearrange("p c t -> p (c t)"), func=COPY, scale=-1.0)
+        interleave_on_scalar(0, 0, 0, N)
+        interleave_on_scalar(0, 1, 0, N)
+        interleave_on_scalar(1, 0, 0, N)
         sort_words(0, 0)
         sort_words(0, 1)
         sort_scales()
-        quantize(0, 0, 1)
+        quantize(0, 0)
         sort_words(1, 0)
-        quantize(0, 1, 2)
+        quantize(0, 1)
         sort_words(1, 1)
+        interleave_on_gpsimd(1)
 
         move_v_scales()
         load_y(1, 0)
@@ -212,41 +222,29 @@ def tile_leapfrog_kick_drift_kick_t2_kernel(tc, z, units, a_words, a_scales, v_w
         load_y(2, 0)
         load_y(2, 1)
 
-        outputs_due = []
-        window = {"step": 0, "steps": 0, "left": 0, "open": False}
+        pieces = []
+        gpsimd_prescales = [(0, PACK), (0, BANKS - 1), (TILES - 1, BANKS - 1)]
 
-        def next_prescale(k):
-            for j in range(TILES - 1):
-                if SLOT_OF[2, j] > k:
-                    for b in range(BANKS):
-                        kept = b == quantize_after(SLOT_OF[2, j])
-                        if (j, b) not in prescaled and not kept and (SLOT_OF[0, j], b // PACK) in interleaved:
-                            return (0, j, b)
-            return None
+        def queue_pieces(k):
+            pieces.extend((k, n0) for n0 in range(0, N, PIECE))
 
-        def gpsimd_turn(k, newest):
-            job = None
-            if not window["open"]:
-                job = newest
-            elif window["step"] % 3 != 0 and window["step"] <= window["steps"] - 2:
-                job = outputs_due[0] if outputs_due else next_prescale(k)
-            if job is not None and window["left"] > 0:
-                if job in outputs_due:
-                    outputs_due.remove(job)
-                scale_rows(False, *job, aside=(job[0] == 0 and not window["open"]))
-                window["open"] = True
-                window["left"] = window["left"] - 1
+        def interleave_pieces(count):
+            for k, n0 in pieces[:count]:
+                interleave_on_scalar(k, 0, n0, n0 + PIECE)
+                pieces.remove((k, n0))
 
         for k, (stage, j) in enumerate(ORDER):
             ahead = k + 2
-            if ahead < SLOTS and source_slot(ahead) != k:
-                for g in range(GROUPS):
-                    interleave(ahead, g)
+            follows = ahead < SLOTS and source_slot(ahead) == k
+            if ahead < SLOTS and source_slot(ahead) is None:
+                queue_pieces(ahead)
+            if stage != 1:
+                interleave_pieces(len(pieces))
             for h in range(GROUPS):
                 if stage == 0:
                     results[k, h] = momenta[j][h]
                 elif stage == 1:
-                    result_tile = ring.tile([P, PACK, N], F32, name="result", bufs=4)
+                    result_tile = ring.tile([P, PACK, N], F32, name="result", bufs=6)
                     results[k, h] = result_tile
                 accs = []
                 if k == 0:
@@ -263,50 +261,40 @@ def tile_leapfrog_kick_drift_kick_t2_kernel(tc, z, units, a_words, a_scales, v_w
                         acc = psum.tile([P, N], F32, name="acc")
                         for g in range(GROUPS):
                             matmul_pass(k, acc, h, t, g)
-                    newest = (stage, j, b)
+                    row = momenta[j][h][:, t, :]
                     if stage == 0:
-                        nc.vector.tensor_tensor(out=results[k, h][:, t, :], in0=y[j][h][:, t, :], in1=acc[:], op=ALU.subtract)
+                        nc.vector.tensor_tensor(out=row, in0=y[j][h][:, t, :], in1=acc[:], op=ALU.subtract)
                     elif stage == 1:
                         nc.vector.tensor_tensor(out=results[k, h][:, t, :], in0=x[j][h][:, t, :], in1=acc[:], op=ALU.add)
-                        if j == TILES - 1 and h == 0:
-                            scale_rows(True, stage, j, b)
-                            newest = None
-                        else:
-                            outputs_due.append(newest)
+                        scale_rows(True, stage, j, b)
                     elif (j, b) in prescaled:
                         nc.vector.scalar_tensor_tensor(
-                            out=momenta[j][h][:, t, :],
-                            in0=acc[:],
-                            scalar=minus_unit_y[:, b : b + 1],
-                            in1=prescaled[j, b],
-                            op0=ALU.mult,
-                            op1=ALU.add,
+                            out=row, in0=acc[:], scalar=minus_unit_y[:, b : b + 1], in1=row, op0=ALU.mult, op1=ALU.add
                         )
                         finish(stage, j, b)
-                        newest = None
                     else:
-                        row = momenta[j][h][:, t, :]
                         nc.vector.tensor_tensor(out=row, in0=row, in1=acc[:], op=ALU.subtract)
-                        outputs_due.append(newest)
-                    if t == PACK - 1 and ahead < SLOTS and source_slot(ahead) == k:
-                        interleave(ahead, h)
-                    window["step"] = window["step"] + 1
+                        scale_rows(True, stage, j, b)
+                    if b == PACK - 1 and stage < STAGES - 1:
+                        queue_pieces(SLOT_OF[stage + 1, j])
+                        if stage == 0:
+                            interleave_pieces(len(pieces))
+                        if k == 0:
+                            nc.scalar.activation(out=unit[:], in_=unit_bf[:].rearrange("p c t -> p (c t)"), func=COPY)
+                            nc.scalar.activation(out=minus_unit_y[:], in_=unit_bf[:, GROUPS:].rearrange("p c t -> p (c t)"), func=COPY, scale=-1.0)
+                            for first in range(PACK):
+                                scale_rows(True, 0, j, first)
                     if k + 1 < SLOTS and b == quantize_after(k):
-                        quantize(k + 1, 0, GROUPS)
-                        if k + 2 < SLOTS:
-                            steps = BANKS - b + quantize_after(k + 1)
-                        else:
-                            steps = 2 * BANKS
-                            for job in [due for due in outputs_due if due != newest]:
-                                outputs_due.remove(job)
-                                scale_rows(True, *job)
-                            for rest in range(BANKS):
-                                if (TILES - 1, rest) not in prescaled:
-                                    scale_rows(True, 0, TILES - 1, rest)
-                        window["step"] = 0
-                        window["steps"] = steps
-                        window["left"] = 2 * steps // 3
-                        window["open"] = False
-                    gpsimd_turn(k, newest)
-        assert not outputs_due
+                        for g in range(GROUPS):
+                            quantize(k + 1, g)
+                        if stage == 1:
+                            interleave_pieces(1)
+                        if ahead < SLOTS and not follows:
+                            interleave_on_gpsimd(ahead)
+                            if quantize_after(k + 1) >= b:
+                                scale_rows(False, 0, *gpsimd_prescales[0])
+                                gpsimd_prescales.remove(gpsimd_prescales[0])
+            if follows:
+                interleave_on_gpsimd(ahead)
+        assert not pieces and not gpsimd_prescales
         assert len(finished) == 2 * TILES * BANKS

@@ -28,16 +28,14 @@ RUN = 4
 SCALE_ROWS = 4
 ORDER = [(0, 0), (0, 1), (1, 0), (0, 2), (1, 1), (1, 2), (2, 0), (2, 1), (2, 2)]
 PIECE = N // 2
+QUANTIZE_AFTER = 5
+HEAD_SHARE = 128
 SLOT_OF = {sj: k for k, sj in enumerate(ORDER)}
 
 
 def source_slot(k):
     stage, j = ORDER[k]
     return SLOT_OF[stage - 1, j] if stage > 0 else None
-
-
-def quantize_after(k):
-    return 5 if k == 0 or source_slot(k + 1) == k - 1 else 4
 
 
 def tile_leapfrog_kick_drift_kick_t2_kernel(tc, z, units, a_words, a_scales, v_words, v_scales, out_0, out_1):
@@ -55,28 +53,26 @@ def tile_leapfrog_kick_drift_kick_t2_kernel(tc, z, units, a_words, a_scales, v_w
         x = [[keep.tile([P, PACK, N], BF16, name="x%d%d" % (j, g)) for g in range(GROUPS)] for j in range(TILES)]
         y = [[keep.tile([P, PACK, N], BF16, name="y%d%d" % (j, g)) for g in range(GROUPS)] for j in range(TILES)]
         momenta = [[keep.tile([P, PACK, N], F32, name="m%d%d" % (j, g)) for g in range(GROUPS)] for j in range(TILES)]
-        raw_v = ring.tile([P, GROUPS, GROUPS, 2 * GROUP], U8, name="packed_late", bufs=1, align_bytes=256)
+        raw_v = ring.tile([P, GROUPS, 2 * D], U8, name="packed_late", bufs=1, align_bytes=256)
         raw_words = [
-            [keep.tile([P, GROUPS, 2 * GROUP], U8, name="rw%d" % h)[:] for h in range(GROUPS)],
-            [raw_v[:, h] for h in range(GROUPS)],
+            [keep.tile([P, 2 * D], U8, name="rw%d" % g)[:] for g in range(GROUPS)],
+            [raw_v[:, g] for g in range(GROUPS)],
         ]
-        words = [[keep.tile([P, GROUPS, 2 * GROUP], U8, name="w%d%d" % (w, h), align_bytes=256) for h in range(GROUPS)] for w in range(2)]
-        raw_scales = keep.tile([P, GROUPS * D], U8, name="rs")
-        scales = [keep.tile([P, GROUPS * D], U8, name="s%d" % w, align_bytes=256) for w in range(2)]
+        words = [[keep.tile([P, 2 * D], U8, name="w%d%d" % (w, g), align_bytes=256) for g in range(GROUPS)] for w in range(2)]
+        raw_scales = [keep.tile([P, D], U8, name="rs%d" % w) for w in range(2)]
+        scales = [[keep.tile([P, D], U8, name="s%d%d" % (w, g), align_bytes=256) for g in range(GROUPS)] for w in range(2)]
         unit_bf = keep.tile([P, 2 * GROUPS, PACK], BF16)
         unit = keep.tile([P, 2 * BANKS], F32)
         minus_unit_y = keep.tile([P, BANKS], F32)
 
-        def load_words(w, h):
-            src = (a_words, v_words)[w][:, :, h * 2 * GROUP : (h + 1) * 2 * GROUP].rearrange("g p n -> p g n")
-            nc.sync.dma_start(out=raw_words[w][h].bitcast(I32), in_=src.bitcast(I32))
+        def load_words(w, g):
+            nc.sync.dma_start(out=raw_words[w][g].bitcast(I32), in_=(a_words, v_words)[w][g].bitcast(I32))
 
-        def load_scales(w, queue):
+        def load_scales(w):
             for q in range(4):
-                first = 32 * q + SCALE_ROWS * w
-                src = (a_scales, v_scales)[w][:, 4 * q : 4 * q + 4, :].rearrange("g r n -> r g n")
-                dst = raw_scales[first : first + SCALE_ROWS, :].rearrange("r (g n) -> r g n", g=GROUPS)
-                queue.dma_start(out=dst.bitcast(I32), in_=src.bitcast(I32))
+                src = (a_scales, v_scales)[w][:, SCALE_ROWS * q : SCALE_ROWS * (q + 1), :]
+                dst = raw_scales[w][32 * q : 32 * q + GROUPS * SCALE_ROWS, :]
+                nc.sync.dma_start(out=dst.bitcast(I32), in_=src.bitcast(I32))
 
         def load_x(j, g):
             nc.sync.dma_start(out=x[j][g][:], in_=rows_of(z, 0, g, j))
@@ -84,23 +80,23 @@ def tile_leapfrog_kick_drift_kick_t2_kernel(tc, z, units, a_words, a_scales, v_w
         def load_y(j, g, t0=0, t1=PACK):
             nc.sync.dma_start(out=y[j][g][:, t0:t1, :], in_=rows_of(z, D, g, j)[:, t0:t1, :])
 
-        def sort_words(w, h):
+        def sort_words(w, g):
             nc.vector.tensor_copy(
-                out=words[w][h][:].rearrange("p g (t m b) -> p g t m b", t=PACK, b=2),
-                in_=raw_words[w][h].rearrange("p g (m t b) -> p g t m b", t=PACK, b=2),
+                out=words[w][g][:].rearrange("p (h t m b) -> p h t m b", h=GROUPS, t=PACK, b=2),
+                in_=raw_words[w][g].rearrange("p (h m t b) -> p h t m b", h=GROUPS, t=PACK, b=2),
             )
 
-        def sort_scales():
+        def sort_scales(w):
             nc.vector.tensor_copy(
-                out=scales[0][:].rearrange("p (c t m) -> p c t m", t=PACK, m=P),
-                in_=raw_scales[:].rearrange("p (c m t) -> p c t m", t=PACK, m=P),
+                out=scales[w][0][:].rearrange("p (c t m) -> p c t m", t=PACK, m=P),
+                in_=raw_scales[w][:].rearrange("p (c m t) -> p c t m", t=PACK, m=P),
             )
 
-        def move_v_scales():
+        def move_scales(w):
             for q in range(4):
                 nc.sync.dma_start(
-                    out=scales[1][32 * q : 32 * q + SCALE_ROWS, :].bitcast(I32),
-                    in_=scales[0][32 * q + SCALE_ROWS : 32 * q + 2 * SCALE_ROWS, :].bitcast(I32),
+                    out=scales[w][1][32 * q : 32 * q + SCALE_ROWS, :].bitcast(I32),
+                    in_=scales[w][0][32 * q + SCALE_ROWS : 32 * q + 2 * SCALE_ROWS, :].bitcast(I32),
                 )
 
         results = {}
@@ -112,11 +108,11 @@ def tile_leapfrog_kick_drift_kick_t2_kernel(tc, z, units, a_words, a_scales, v_w
         def operand_rows(k, g):
             return x[ORDER[k][1]][g] if source_slot(k) is None else results[source_slot(k), g]
 
-        def interleave_on_scalar(k, g, n0, n1):
+        def interleave(copy, k, g, n0, n1):
             if n0 == 0:
                 tile = ring.tile([P, N, PACK], BF16, name="packed_early", bufs=4, align_bytes=256)
                 packed[k, g] = tile
-            nc.scalar.copy(
+            copy(
                 out=packed[k, g][:, n0:n1, :].rearrange("p (c i) t -> p c t i", i=RUN),
                 in_=operand_rows(k, g)[:, :, n0:n1].rearrange("p t (c i) -> p c t i", i=RUN),
             )
@@ -142,11 +138,11 @@ def tile_leapfrog_kick_drift_kick_t2_kernel(tc, z, units, a_words, a_scales, v_w
 
         def matmul_pass(k, acc, h, t, g):
             w = ORDER[k][0] % 2
-            first = (g * BANKS + h * PACK + t) * P
+            column = (h * PACK + t) * P
             nc.tensor.matmul_mx(
                 out=acc[:],
-                lhsT=words[w][h][:, g, t * 2 * P : (t + 1) * 2 * P].bitcast(FP4X4),
-                lhsT_scale=scales[w][:, first : first + P],
+                lhsT=words[w][g][:, 2 * column : 2 * (column + P)].bitcast(FP4X4),
+                lhsT_scale=scales[w][g][:, column : column + P],
                 rhs=codes[k][:, g * N : (g + 1) * N].bitcast(FP8X4),
                 rhs_scale=code_scales[k][:, g * N : (g + 1) * N],
                 start=(g == 0),
@@ -185,52 +181,50 @@ def tile_leapfrog_kick_drift_kick_t2_kernel(tc, z, units, a_words, a_scales, v_w
             else:
                 finish(stage, j, b)
 
-        nc.vector.memset(raw_scales[:].bitcast(I32), 0)
-        nc.vector.memset(scales[1][:].bitcast(I32), 0)
+        nc.gpsimd.memset(raw_scales[0][:].bitcast(I32), 0)
+        for plane in (scales[0][1], raw_scales[1], scales[1][1]):
+            nc.vector.memset(plane[:].bitcast(I32), 0)
         load_words(0, 0)
         load_x(0, 0)
-        load_scales(0, nc.scalar)
+        load_scales(0)
         load_words(0, 1)
-        load_scales(1, nc.sync)
         load_x(0, 1)
         load_words(1, 0)
         load_words(1, 1)
+        sort_words(0, 0)
+        sort_scales(0)
+        move_scales(0)
         load_x(1, 0)
         load_y(0, 0, 0, PACK // 2)
         load_x(1, 1)
         load_y(0, 0, PACK // 2, PACK)
         load_y(0, 1)
+        load_scales(1)
         nc.sync.dma_start(out=unit_bf[:], in_=units.rearrange("(c p t) -> p c t", p=P, t=PACK))
+        load_y(1, 0)
+        load_x(2, 0)
+        load_y(1, 1)
 
-        interleave_on_scalar(0, 0, 0, N)
-        interleave_on_scalar(0, 1, 0, N)
-        interleave_on_scalar(1, 0, 0, N)
-        sort_words(0, 0)
+        interleave(nc.scalar.copy, 0, 0, 0, N)
+        interleave(nc.scalar.copy, 0, 1, 0, N - HEAD_SHARE)
+        interleave(nc.scalar.copy, 1, 0, 0, N)
         sort_words(0, 1)
-        sort_scales()
         quantize(0, 0)
+        interleave(nc.vector.tensor_copy, 0, 1, N - HEAD_SHARE, N)
         sort_words(1, 0)
         quantize(0, 1)
         sort_words(1, 1)
         interleave_on_gpsimd(1)
 
-        move_v_scales()
-        load_y(1, 0)
-        load_x(2, 0)
-        load_y(1, 1)
-        load_x(2, 1)
-        load_y(2, 0)
-        load_y(2, 1)
-
         pieces = []
-        gpsimd_prescales = [(0, PACK), (0, BANKS - 1), (TILES - 1, BANKS - 1)]
+        gpsimd_prescales = list(range(PACK, BANKS))
 
         def queue_pieces(k):
             pieces.extend((k, n0) for n0 in range(0, N, PIECE))
 
         def interleave_pieces(count):
-            for k, n0 in pieces[:count]:
-                interleave_on_scalar(k, 0, n0, n0 + PIECE)
+            for k, n0 in sorted(pieces)[:count]:
+                interleave(nc.scalar.copy, k, 0, n0, n0 + PIECE)
                 pieces.remove((k, n0))
 
         for k, (stage, j) in enumerate(ORDER):
@@ -238,8 +232,14 @@ def tile_leapfrog_kick_drift_kick_t2_kernel(tc, z, units, a_words, a_scales, v_w
             follows = ahead < SLOTS and source_slot(ahead) == k
             if ahead < SLOTS and source_slot(ahead) is None:
                 queue_pieces(ahead)
-            if stage != 1:
                 interleave_pieces(len(pieces))
+            if (stage, j) == (STAGES - 1, 0):
+                for b in range(QUANTIZE_AFTER + 1):
+                    scale_rows(True, 0, 1, b)
+                interleave_pieces(len(pieces))
+                for b in range(QUANTIZE_AFTER + 1, 2 * BANKS):
+                    scale_rows(True, 0, 1 + b // BANKS, b % BANKS)
+            groups_apart = k == 0
             for h in range(GROUPS):
                 if stage == 0:
                     results[k, h] = momenta[j][h]
@@ -247,14 +247,14 @@ def tile_leapfrog_kick_drift_kick_t2_kernel(tc, z, units, a_words, a_scales, v_w
                     result_tile = ring.tile([P, PACK, N], F32, name="result", bufs=6)
                     results[k, h] = result_tile
                 accs = []
-                if k == 0:
+                if groups_apart and h == 0:
                     for t in range(PACK):
                         acc = psum.tile([P, N], F32, name="acc")
                         accs.append(acc)
                         matmul_pass(k, acc, h, t, 0)
                 for t in range(PACK):
                     b = h * PACK + t
-                    if k == 0:
+                    if groups_apart and h == 0:
                         acc = accs[t]
                         matmul_pass(k, acc, h, t, 1)
                     else:
@@ -267,14 +267,11 @@ def tile_leapfrog_kick_drift_kick_t2_kernel(tc, z, units, a_words, a_scales, v_w
                     elif stage == 1:
                         nc.vector.tensor_tensor(out=results[k, h][:, t, :], in0=x[j][h][:, t, :], in1=acc[:], op=ALU.add)
                         scale_rows(True, stage, j, b)
-                    elif (j, b) in prescaled:
+                    else:
                         nc.vector.scalar_tensor_tensor(
                             out=row, in0=acc[:], scalar=minus_unit_y[:, b : b + 1], in1=row, op0=ALU.mult, op1=ALU.add
                         )
                         finish(stage, j, b)
-                    else:
-                        nc.vector.tensor_tensor(out=row, in0=row, in1=acc[:], op=ALU.subtract)
-                        scale_rows(True, stage, j, b)
                     if b == PACK - 1 and stage < STAGES - 1:
                         queue_pieces(SLOT_OF[stage + 1, j])
                         if stage == 0:
@@ -284,17 +281,23 @@ def tile_leapfrog_kick_drift_kick_t2_kernel(tc, z, units, a_words, a_scales, v_w
                             nc.scalar.activation(out=minus_unit_y[:], in_=unit_bf[:, GROUPS:].rearrange("p c t -> p (c t)"), func=COPY, scale=-1.0)
                             for first in range(PACK):
                                 scale_rows(True, 0, j, first)
-                    if k + 1 < SLOTS and b == quantize_after(k):
+                    if k + 1 < SLOTS and b == QUANTIZE_AFTER:
+                        if k == 0:
+                            sort_scales(1)
+                            move_scales(1)
+                            load_x(2, 1)
+                            load_y(2, 0)
+                            load_y(2, 1)
                         for g in range(GROUPS):
                             quantize(k + 1, g)
                         if stage == 1:
                             interleave_pieces(1)
                         if ahead < SLOTS and not follows:
                             interleave_on_gpsimd(ahead)
-                            if quantize_after(k + 1) >= b:
-                                scale_rows(False, 0, *gpsimd_prescales[0])
+                            if gpsimd_prescales:
+                                scale_rows(False, 0, 0, gpsimd_prescales[0])
                                 gpsimd_prescales.remove(gpsimd_prescales[0])
             if follows:
                 interleave_on_gpsimd(ahead)
-        assert not pieces and not gpsimd_prescales
+        assert not pieces and len(prescaled) == TILES * BANKS
         assert len(finished) == 2 * TILES * BANKS

from contextlib import ExitStack

import concourse.mybir as mybir

D, B = 1024, 1536
FLOPS = 3 * 2 * D * D * B

F32 = mybir.dt.float32
BF16 = mybir.dt.bfloat16
I32 = mybir.dt.int32
U32 = mybir.dt.uint32
U8 = mybir.dt.uint8
FP8X4 = mybir.dt.float8_e4m3fn_x4
FP4X4 = mybir.dt.float4_e2m1fn_x4
ALU = mybir.AluOpType
COPY = mybir.ActivationFunctionType.Copy

P = 128
PACK = 4
GROUP = P * PACK
GROUPS = D // GROUP
N = 512
TILES = B // N
STAGES = 3
SLOTS = STAGES * TILES
BANKS = GROUPS * PACK
RUN = 4
SCALE_ROWS = 4
ORDER = [(0, 0), (0, 1), (1, 0), (0, 2), (1, 1), (1, 2), (2, 0), (2, 1), (2, 2)]
PIECE = N // 2
QUANTIZE_AFTER = 5
HEAD_SHARE = 128
SLOT_OF = {sj: k for k, sj in enumerate(ORDER)}


def source_slot(k):
    stage, j = ORDER[k]
    return SLOT_OF[stage - 1, j] if stage > 0 else None


def tile_leapfrog_kick_drift_kick_t2_kernel(tc, z, units, a_words, a_scales, v_words, v_scales, out_0, out_1):
    nc = tc.nc

    def rows_of(dram, base, g, j):
        return dram[base + g * GROUP : base + (g + 1) * GROUP, j * N : (j + 1) * N].rearrange("(p t) n -> p t n", t=PACK)

    with ExitStack() as ctx:
        keep = ctx.enter_context(tc.tile_pool(name="keep", bufs=1))
        ring = ctx.enter_context(tc.tile_pool(name="ring", bufs=2))
        psum = ctx.enter_context(tc.psum_pool(name="psum", bufs=BANKS))
        ctx.enter_context(tc.manual_schedule())

        x = [[keep.tile([P, PACK, N], BF16, name="x%d%d" % (j, g)) for g in range(GROUPS)] for j in range(TILES)]
        y = [[keep.tile([P, PACK, N], BF16, name="y%d%d" % (j, g)) for g in range(GROUPS)] for j in range(TILES)]
        momenta = [[keep.tile([P, PACK, N], F32, name="m%d%d" % (j, g)) for g in range(GROUPS)] for j in range(TILES)]
        raw_v = ring.tile([P, GROUPS, 2 * D], U8, name="packed_late", bufs=1, align_bytes=256)
        raw_words = [
            [keep.tile([P, 2 * D], U8, name="rw%d" % g)[:] for g in range(GROUPS)],
            [raw_v[:, g] for g in range(GROUPS)],
        ]
        words = [[keep.tile([P, 2 * D], U8, name="w%d%d" % (w, g), align_bytes=256) for g in range(GROUPS)] for w in range(2)]
        raw_scales = [keep.tile([P, D], U8, name="rs%d" % w) for w in range(2)]
        scales = [[keep.tile([P, D], U8, name="s%d%d" % (w, g), align_bytes=256) for g in range(GROUPS)] for w in range(2)]
        unit_bf = keep.tile([P, 2 * GROUPS, PACK], BF16)
        unit = keep.tile([P, 2 * BANKS], F32)
        minus_unit_y = keep.tile([P, BANKS], F32)

        def load_words(w, g):
            nc.sync.dma_start(out=raw_words[w][g].bitcast(I32), in_=(a_words, v_words)[w][g].bitcast(I32))

        def load_scales(w):
            for q in range(4):
                src = (a_scales, v_scales)[w][:, SCALE_ROWS * q : SCALE_ROWS * (q + 1), :]
                dst = raw_scales[w][32 * q : 32 * q + GROUPS * SCALE_ROWS, :]
                nc.sync.dma_start(out=dst.bitcast(I32), in_=src.bitcast(I32))

        def load_x(j, g):
            nc.sync.dma_start(out=x[j][g][:], in_=rows_of(z, 0, g, j))

        def load_y(j, g, t0=0, t1=PACK):
            nc.sync.dma_start(out=y[j][g][:, t0:t1, :], in_=rows_of(z, D, g, j)[:, t0:t1, :])

        def sort_words(w, g):
            nc.vector.tensor_copy(
                out=words[w][g][:].rearrange("p (h t m b) -> p h t m b", h=GROUPS, t=PACK, b=2),
                in_=raw_words[w][g].rearrange("p (h m t b) -> p h t m b", h=GROUPS, t=PACK, b=2),
            )

        def sort_scales(w):
            nc.vector.tensor_copy(
                out=scales[w][0][:].rearrange("p (c t m) -> p c t m", t=PACK, m=P),
                in_=raw_scales[w][:].rearrange("p (c m t) -> p c t m", t=PACK, m=P),
            )

        def move_scales(w):
            for q in range(4):
                nc.sync.dma_start(
                    out=scales[w][1][32 * q : 32 * q + SCALE_ROWS, :].bitcast(I32),
                    in_=scales[w][0][32 * q + SCALE_ROWS : 32 * q + 2 * SCALE_ROWS, :].bitcast(I32),
                )

        results = {}
        packed = {}
        codes = {}
        code_scales = {}
        staged = {}

        def operand_rows(k, g):
            return x[ORDER[k][1]][g] if source_slot(k) is None else results[source_slot(k), g]

        def interleave(copy, k, g, n0, n1):
            if n0 == 0:
                tile = ring.tile([P, N, PACK], BF16, name="packed_early", bufs=4, align_bytes=256)
                packed[k, g] = tile
            copy(
                out=packed[k, g][:, n0:n1, :].rearrange("p (c i) t -> p c t i", i=RUN),
                in_=operand_rows(k, g)[:, :, n0:n1].rearrange("p t (c i) -> p c t i", i=RUN),
            )

        def interleave_on_gpsimd(k):
            tile = ring.tile([P, N, PACK], BF16, name="packed_late", bufs=1, align_bytes=256)
            packed[k, 1] = tile
            nc.gpsimd.tensor_scalar(
                out=tile[:], in0=operand_rows(k, 1)[:].rearrange("p t n -> p n t"), scalar1=1.0, scalar2=0.0, op0=ALU.mult, op1=ALU.add
            )

        def quantize(k, g):
            if g == 0:
                code_tile = ring.tile([P, GROUPS * N], U32, name="codes", bufs=3, align_bytes=256)
                scale_tile = ring.tile([P, GROUPS * N], U8, name="code_scales", bufs=3, align_bytes=256)
                codes[k] = code_tile
                code_scales[k] = scale_tile
            nc.vector.quantize_mx(
                out=codes[k][:, g * N : (g + 1) * N].bitcast(FP8X4),
                scales=code_scales[k][:, g * N : (g + 1) * N],
                in_=packed[k, g][:].rearrange("p n t -> p (n t)"),
            )

        def matmul_pass(k, acc, h, t, g):
            w = ORDER[k][0] % 2
            column = (h * PACK + t) * P
            nc.tensor.matmul_mx(
                out=acc[:],
                lhsT=words[w][g][:, 2 * column : 2 * (column + P)].bitcast(FP4X4),
                lhsT_scale=scales[w][g][:, column : column + P],
                rhs=codes[k][:, g * N : (g + 1) * N].bitcast(FP8X4),
                rhs_scale=code_scales[k][:, g * N : (g + 1) * N],
                start=(g == 0),
                stop=(g == GROUPS - 1),
            )

        finished = set()

        def finish(stage, j, b):
            h, t = divmod(b, PACK)
            dram, tile = (out_0, staged[j, h]) if stage == 1 else (out_1, momenta[j][h])
            finished.add((stage, j, b))
            if SLOT_OF[stage, j] == SLOTS - 1 and b >= BANKS - 2:
                nc.sync.dma_start(out=rows_of(dram, 0, h, j)[:, t : t + 1, :], in_=tile[:, t : t + 1, :])
            elif (stage, j, b ^ 1) in finished:
                t0 = t - t % 2
                nc.sync.dma_start(out=rows_of(dram, 0, h, j)[:, t0 : t0 + 2, :], in_=tile[:, t0 : t0 + 2, :])

        prescaled = set()

        def scale_rows(on_scalar, stage, j, b):
            h, t = divmod(b, PACK)
            if stage == 1:
                if t == 0:
                    out_tile = ring.tile([P, PACK, N], F32, name="staged", bufs=4)
                    staged[j, h] = out_tile
                src, dst, col = results[SLOT_OF[1, j], h][:, t, :], staged[j, h][:, t, :], b
            else:
                src, dst, col = momenta[j][h][:, t, :], momenta[j][h][:, t, :], BANKS + b
            if on_scalar:
                nc.scalar.activation(out=dst, in_=src, func=COPY, scale=unit[:, col : col + 1])
            else:
                nc.gpsimd.tensor_scalar(out=dst, in0=src, scalar1=unit[:, col : col + 1], scalar2=0.0, op0=ALU.mult, op1=ALU.add)
            if stage == 0:
                prescaled.add((j, b))
            else:
                finish(stage, j, b)

        nc.gpsimd.memset(raw_scales[0][:].bitcast(I32), 0)
        for plane in (scales[0][1], raw_scales[1], scales[1][1]):
            nc.vector.memset(plane[:].bitcast(I32), 0)
        load_words(0, 0)
        load_x(0, 0)
        load_scales(0)
        load_words(0, 1)
        load_x(0, 1)
        load_words(1, 0)
        load_words(1, 1)
        sort_words(0, 0)
        sort_scales(0)
        move_scales(0)
        load_x(1, 0)
        load_y(0, 0, 0, PACK // 2)
        load_x(1, 1)
        load_y(0, 0, PACK // 2, PACK)
        load_y(0, 1)
        load_scales(1)
        nc.sync.dma_start(out=unit_bf[:], in_=units.rearrange("(c p t) -> p c t", p=P, t=PACK))
        load_y(1, 0)
        load_x(2, 0)
        load_y(1, 1)

        interleave(nc.scalar.copy, 0, 0, 0, N)
        interleave(nc.scalar.copy, 0, 1, 0, N - HEAD_SHARE)
        interleave(nc.scalar.copy, 1, 0, 0, N)
        sort_words(0, 1)
        quantize(0, 0)
        interleave(nc.vector.tensor_copy, 0, 1, N - HEAD_SHARE, N)
        sort_words(1, 0)
        quantize(0, 1)
        sort_words(1, 1)
        interleave_on_gpsimd(1)

        pieces = []
        gpsimd_prescales = list(range(PACK, BANKS))

        def queue_pieces(k):
            pieces.extend((k, n0) for n0 in range(0, N, PIECE))

        def interleave_pieces(count):
            for k, n0 in sorted(pieces)[:count]:
                interleave(nc.scalar.copy, k, 0, n0, n0 + PIECE)
                pieces.remove((k, n0))

        for k, (stage, j) in enumerate(ORDER):
            ahead = k + 2
            follows = ahead < SLOTS and source_slot(ahead) == k
            if ahead < SLOTS and source_slot(ahead) is None:
                queue_pieces(ahead)
                interleave_pieces(len(pieces))
            if (stage, j) == (STAGES - 1, 0):
                for b in range(QUANTIZE_AFTER + 1):
                    scale_rows(True, 0, 1, b)
                interleave_pieces(len(pieces))
                for b in range(QUANTIZE_AFTER + 1, 2 * BANKS):
                    scale_rows(True, 0, 1 + b // BANKS, b % BANKS)
            groups_apart = k == 0
            for h in range(GROUPS):
                if stage == 0:
                    results[k, h] = momenta[j][h]
                elif stage == 1:
                    result_tile = ring.tile([P, PACK, N], F32, name="result", bufs=6)
                    results[k, h] = result_tile
                accs = []
                if groups_apart and h == 0:
                    for t in range(PACK):
                        acc = psum.tile([P, N], F32, name="acc")
                        accs.append(acc)
                        matmul_pass(k, acc, h, t, 0)
                for t in range(PACK):
                    b = h * PACK + t
                    if groups_apart and h == 0:
                        acc = accs[t]
                        matmul_pass(k, acc, h, t, 1)
                    else:
                        acc = psum.tile([P, N], F32, name="acc")
                        for g in range(GROUPS):
                            matmul_pass(k, acc, h, t, g)
                    row = momenta[j][h][:, t, :]
                    if stage == 0:
                        nc.vector.tensor_tensor(out=row, in0=y[j][h][:, t, :], in1=acc[:], op=ALU.subtract)
                    elif stage == 1:
                        nc.vector.tensor_tensor(out=results[k, h][:, t, :], in0=x[j][h][:, t, :], in1=acc[:], op=ALU.add)
                        scale_rows(True, stage, j, b)
                    else:
                        nc.vector.scalar_tensor_tensor(
                            out=row, in0=acc[:], scalar=minus_unit_y[:, b : b + 1], in1=row, op0=ALU.mult, op1=ALU.add
                        )
                        finish(stage, j, b)
                    if b == PACK - 1 and stage < STAGES - 1:
                        queue_pieces(SLOT_OF[stage + 1, j])
                        if stage == 0:
                            interleave_pieces(len(pieces))
                        if k == 0:
                            nc.scalar.activation(out=unit[:], in_=unit_bf[:].rearrange("p c t -> p (c t)"), func=COPY)
                            nc.scalar.activation(out=minus_unit_y[:], in_=unit_bf[:, GROUPS:].rearrange("p c t -> p (c t)"), func=COPY, scale=-1.0)
                            for first in range(PACK):
                                scale_rows(True, 0, j, first)
                    if k + 1 < SLOTS and b == QUANTIZE_AFTER:
                        if k == 0:
                            sort_scales(1)
                            move_scales(1)
                            load_x(2, 1)
                            load_y(2, 0)
                            load_y(2, 1)
                        for g in range(GROUPS):
                            quantize(k + 1, g)
                        if stage == 1:
                            interleave_pieces(1)
                        if ahead < SLOTS and not follows:
                            interleave_on_gpsimd(ahead)
                            if gpsimd_prescales:
                                scale_rows(False, 0, 0, gpsimd_prescales[0])
                                gpsimd_prescales.remove(gpsimd_prescales[0])
            if follows:
                interleave_on_gpsimd(ahead)
        assert not pieces and len(prescaled) == TILES * BANKS
        assert len(finished) == 2 * TILES * BANKS
